import numpy as np
import ml_dtypes


def mxq(x, axis, fmt="e4m3"):
    dtype, down = {"e4m3": (ml_dtypes.float8_e4m3fn, 7), "e5m2": (ml_dtypes.float8_e5m2, 14)}[fmt]
    v = np.moveaxis(np.asarray(x, np.float32).astype(ml_dtypes.bfloat16).astype(np.float64), axis, -1)
    blocks = v.reshape(v.shape[:-1] + (-1, 32))
    amax = np.abs(blocks).max(-1, keepdims=True)
    byte = np.maximum(np.where(amax > 0, np.frexp(amax)[1] - 1 + 127, 0) - down, 1)
    scale = np.exp2(byte - 127.0)
    codes = (blocks / scale).astype(np.float32).astype(dtype).astype(np.float64)
    return np.moveaxis((codes * scale).reshape(v.shape), -1, axis)


WIDE = False


def mx_kscale(k):
    if not WIDE:
        return np.ones(k)
    levels = np.array([10, -10, 5, -5, 0])
    if k % 512:
        return np.exp2(np.random.permutation(np.resize(levels, k // 32))).repeat(32)
    a = np.empty((k // 512, 16))
    for p in range(k // 512):
        a[p, :8] = np.random.permutation(np.resize(levels, 8))
        for g in range(8):
            far = levels[np.abs(levels - a[p, g]) >= 10]
            a[p, g + 8] = far[np.random.randint(len(far))]
    return np.exp2(a.ravel()).repeat(32)


def f64(x):
    return np.asarray(x).astype(np.float64)


def striped(idx):
    return np.tile(idx.reshape(-1, 16).T, (8, 1)).astype(np.uint16)


def unstriped(offs):
    return offs[:16].T.reshape(-1).astype(np.int64)


E2M1 = np.array([0.0, 0.5, 1.0, 1.5, 2.0, 3.0, 4.0, 6.0, -0.0, -0.5, -1.0, -1.5, -2.0, -3.0, -4.0, -6.0])


def pack_weight(w, fmt):
    k, n = w.shape
    w = f64(np.asarray(w, np.float32).astype(ml_dtypes.bfloat16)).reshape(k // 32, 32, n)
    amax = np.abs(w).max(1)
    if fmt == "e4m3":
        byte = np.frexp(amax)[1] - 1 + 127 - 7
    else:
        mant, ex = np.frexp(amax / 6.0)
        byte = np.where(mant > 0.5, ex, ex - 1) + 127
    byte = np.clip(np.where(amax > 0, byte, 1), 1, 254)
    scaled = (w * np.exp2(127.0 - byte)[:, None, :]).reshape(k, n).astype(np.float32)
    by_word = np.ascontiguousarray(scaled.reshape(k // 512, 128, 4, n).transpose(0, 1, 3, 2))
    if fmt == "e4m3":
        words = by_word.astype(ml_dtypes.float8_e4m3fn).view(np.uint8)
    else:
        c = by_word.astype(ml_dtypes.float4_e2m1fn).view(np.uint8) & 0xF
        words = (c[..., 0::2] | (c[..., 1::2] << 4)).reshape(k // 512, 128, 2 * n)
    return np.ascontiguousarray(words), np.ascontiguousarray(byte.astype(np.uint8).reshape(k // 512, 16, n))


def unpack_weight(words, scales, fmt):
    g, _, n = scales.shape
    words = np.ascontiguousarray(words).reshape(g, 128, n, -1)
    if fmt == "e4m3":
        vals = words.view(ml_dtypes.float8_e4m3fn).astype(np.float64)
    else:
        nib = np.empty((g, 128, n, 4), np.uint8)
        nib[..., 0::2] = words & 0xF
        nib[..., 1::2] = words >> 4
        vals = E2M1[nib]
    vals = vals * np.repeat(np.exp2(scales.astype(np.float64) - 127.0), 8, axis=1)[..., None]
    return vals.transpose(0, 1, 3, 2).reshape(g * 512, n)


def sigmoid(v):
    return 1.0 / (1.0 + np.exp(-np.maximum(v, -700.0)))


K, T, E, C, H, N = 512, 512, 6, 256, 512, 128
TOP = 3


def by_expert(wq, xq):
    return np.concatenate([wq[e].T @ xq[:, e * C:(e + 1) * C] for e in range(E)], axis=1)


def setup_inputs():
    n = np.random.standard_normal
    s = mx_kscale(K)[:, None]
    u = mx_kscale(H)
    deal = np.repeat(np.arange(E), C).reshape(TOP, T)[:, np.random.permutation(T)]
    deal = np.take_along_axis(deal, np.argsort(np.random.rand(TOP, T), axis=0), axis=0)
    for _ in range(8):
        s_, t_ = np.random.permutation(T).reshape(2, -1); r = np.random.randint(TOP, size=T // 2); x, y = deal[r, s_].copy(), deal[r, t_].copy()
        ok = ~((deal[:, s_] == y).any(0) | (deal[:, t_] == x).any(0)); deal[r[ok], s_[ok]] = y[ok]; deal[r[ok], t_[ok]] = x[ok]
    order = np.lexsort((np.random.rand(TOP * T), deal.reshape(-1)))
    slot_token = order % T; pos = np.empty(TOP * T, np.int64); pos[order] = np.arange(TOP * T); pos = pos.reshape(TOP, T)
    g = np.random.uniform(0.5, 1.5, (TOP, T)); g = g / g.sum(0)
    w1 = [pack_weight(m, "e2m1") for m in n((E, K, H)) / np.sqrt(K) / s[None]]
    w3 = [pack_weight(m, "e2m1") for m in n((E, K, H)) / np.sqrt(K) / s[None] * u[None, None, :]]
    w2 = [pack_weight(m, "e2m1") for m in n((E, H, N)) / np.sqrt(H) / u[None, :, None]]
    return {
        "xT": (n((K, T)) * s).astype(np.float32),
        "w1_words": np.stack([m[0] for m in w1]),
        "w1_scales": np.stack([m[1] for m in w1]),
        "w3_words": np.stack([m[0] for m in w3]),
        "w3_scales": np.stack([m[1] for m in w3]),
        "w2_words": np.stack([m[0] for m in w2]),
        "w2_scales": np.stack([m[1] for m in w2]),
        "gate": np.stack([np.tile(r, (N, 1)) for r in g]).astype(np.float32),
        "offs": striped(slot_token),
        "pos1": striped(pos[0]),
        "pos2": striped(pos[1]),
        "pos3": striped(pos[2]),
    }


def reference(xT, w1_words, w1_scales, w3_words, w3_scales, w2_words, w2_scales, gate, offs, pos1, pos2, pos3):
    idx = unstriped(offs)
    w1 = np.stack([unpack_weight(w1_words[e], w1_scales[e], "e2m1") for e in range(E)])
    w3 = np.stack([unpack_weight(w3_words[e], w3_scales[e], "e2m1") for e in range(E)])
    w2 = np.stack([unpack_weight(w2_words[e], w2_scales[e], "e2m1") for e in range(E)])
    xq = mxq(f64(xT)[:, idx], 0, "e4m3")
    h = sigmoid(by_expert(w1, xq))
    h = h * by_expert(w3, xq)
    y = by_expert(w2, mxq(h, 0, "e4m3"))
    return sum(f64(gate[r]) * y[:, unstriped(p)] for r, p in enumerate((pos1, pos2, pos3)))

@@ -1,0 +1,201 @@
+from contextlib import ExitStack
+
+import concourse.mybir as mybir
+from concourse.masks import make_identity
+
+P = 128
+K, T, E, C, H, N = 512, 512, 6, 256, 512, 128
+S = E * C
+TOP = 3
+FLOPS = 2 * S * (2 * K * H + H * N)
+
+F32 = mybir.dt.float32
+BF16 = mybir.dt.bfloat16
+I32 = mybir.dt.int32
+U32 = mybir.dt.uint32
+U16 = mybir.dt.uint16
+U8 = mybir.dt.uint8
+FP8X4 = mybir.dt.float8_e4m3fn_x4
+FP4X4 = mybir.dt.float4_e2m1fn_x4
+SIGMOID = mybir.ActivationFunctionType.Sigmoid
+MULT = mybir.AluOpType.mult
+ADD = mybir.AluOpType.add
+
+
+def tile_moe_tk_glu_sigmoid_kernel(
+    tc, xT, w1_words, w1_scales, w3_words, w3_scales, w2_words, w2_scales, gate, offs, pos1, pos2, pos3, out
+):
+    nc = tc.nc
+    with ExitStack() as ctx:
+        keep = ctx.enter_context(tc.tile_pool(name="keep", bufs=1))
+        work = ctx.enter_context(tc.tile_pool(name="work", bufs=3))
+        psum = ctx.enter_context(tc.psum_pool(name="psum", bufs=2))
+
+        warm = keep.tile([P, 1], F32, name="warm")
+        nc.vector.memset(warm[:], 0.0)
+        warm2 = keep.tile([P, 1], F32, name="warm2")
+        nc.scalar.activation(warm2[:], warm[:], SIGMOID)
+
+        x_view = xT.rearrange("(p j) t -> p j t", j=4)
+        x_raw = []
+        offs_t = keep.tile([P, S // 16], U16, name="offs_t")
+        nc.sync.dma_start(offs_t[:], offs)
+        x_cuts = [(0, 256), (256, 512)]
+        for c, (t0, t1) in enumerate(x_cuts):
+            xr = keep.tile([P, 4, t1 - t0], F32, name=f"x_raw{c}")
+            nc.sync.dma_start(out=xr[:], in_=x_view[:, :, t0:t1])
+            x_raw.append(xr)
+
+        sc1 = keep.tile([P, E * H], U8, align_bytes=64, name="sc1")
+        sc3 = keep.tile([P, E * H], U8, align_bytes=64, name="sc3")
+        sc2 = keep.tile([P, E * N], U8, align_bytes=64, name="sc2")
+        xs = keep.tile([P, T], U8, align_bytes=64, name="xs")
+        nc.vector.memset(sc1[:].bitcast(I32), 0)
+        nc.vector.memset(sc3[:].bitcast(I32), 0)
+        nc.vector.memset(sc2[:].bitcast(I32), 0)
+        nc.gpsimd.memset(xs[:], 0)
+
+        def load_words(words, width, e0, e1, name, eng):
+            t = keep.tile([P, (e1 - e0) * 2 * width], U8, align_bytes=64, name=name)
+            src = words.bitcast(I32)[e0:e1, 0].rearrange("e p c -> p e c")
+            eng.dma_start(out=t[:].bitcast(I32).rearrange("p (e c) -> p e c", e=e1 - e0), in_=src)
+            return [t[:, i * 2 * width : (i + 1) * 2 * width] for i in range(e1 - e0)]
+
+        def load_scales(tile, scales, eng):
+            src = scales.bitcast(I32)
+            for q in range(4):
+                eng.dma_start(
+                    out=tile[:].bitcast(I32)[32 * q : 32 * q + 4, :].rearrange("p (e c) -> p e c", e=E),
+                    in_=src[:, 0, 4 * q : 4 * q + 4, :].rearrange("e q c -> q e c"),
+                )
+
+        w1 = load_words(w1_words, H, 0, 1, "w1_a", nc.gpsimd)
+        w3 = load_words(w3_words, H, 0, 1, "w3_a", nc.gpsimd)
+        load_scales(sc1, w1_scales, nc.sync)
+        load_scales(sc3, w3_scales, nc.sync)
+        load_scales(sc2, w2_scales, nc.sync)
+        ident = keep.tile([P, P], F32, name="ident")
+        make_identity(nc, ident[:])
+        w1 += load_words(w1_words, H, 1, 3, "w1_b", nc.gpsimd)
+        w3 += load_words(w3_words, H, 1, 3, "w3_b", nc.gpsimd)
+        w2 = load_words(w2_words, N, 0, E, "w2_t", nc.gpsimd)
+        w1 += load_words(w1_words, H, 3, 6, "w1_c", nc.sync)
+        w3 += load_words(w3_words, H, 3, 6, "w3_c", nc.sync)
+        pos_t = []
+        for r, pos in enumerate((pos1, pos2, pos3)):
+            pt = keep.tile([P, T // 16], U16, name=f"pos_t{r}")
+            nc.sync.dma_start(pt[:], pos)
+            pos_t.append(pt)
+        gate_t = keep.tile([P, TOP, T], F32, name="gate_t")
+        nc.sync.dma_start(out=gate_t[:], in_=gate.rearrange("r p t -> p r t"))
+
+        xw = keep.tile([P, T], U32, align_bytes=64, name="xw")
+        for c, (t0, t1) in enumerate(x_cuts):
+            xb = keep.tile([P, t1 - t0, 4], BF16, align_bytes=64, name=f"x_bf{c}")
+            nc.vector.tensor_copy(out=xb[:], in_=x_raw[c][:].rearrange("p j t -> p t j"))
+            cols = slice(t0, t1)
+            nc.vector.quantize_mx(
+                out=xw[:, cols].bitcast(FP8X4), scales=xs[:, cols], in_=xb[:].rearrange("p t j -> p (t j)")
+            )
+
+        y_all = keep.tile([P, S], F32, name="y_all")
+        gw = {}
+        gs = {}
+        h_bf = {}
+        ht_ps = {}
+
+        def gather(e, pieces):
+            a = keep.tile([P, C], U32, align_bytes=64, name=f"gw{e}")
+            b = keep.tile([P, C], U8, align_bytes=64, name=f"gs{e}")
+            n = C // pieces
+            for i in range(pieces):
+                idx = offs_t[:, (e * C + i * n) // 16 : (e * C + (i + 1) * n) // 16]
+                nc.vector.tensor_copy(a[:, i * n : (i + 1) * n], xw[:].indirect(idx))
+                nc.vector.tensor_copy(b[:, i * n : (i + 1) * n], xs[:].indirect(idx))
+            gw[e] = a
+            gs[e] = b
+
+        def first(e, s):
+            cols = slice(s * P, (s + 1) * P)
+            res = []
+            for w, sc, nm in ((w1, sc1, "a_ps"), (w3, sc3, "b_ps")):
+                ps = psum.tile([P, H], F32, name=nm)
+                nc.tensor.matmul_mx(
+                    out=ps[:],
+                    lhsT=gw[e][:, cols].bitcast(FP8X4),
+                    lhsT_scale=gs[e][:, cols],
+                    rhs=w[e].bitcast(FP4X4),
+                    rhs_scale=sc[:, e * H : (e + 1) * H],
+                    start=True,
+                    stop=True,
+                )
+                res.append(ps)
+            sig = work.tile([P, H], F32, name="sig")
+            nc.scalar.activation(sig[:], res[0][:], SIGMOID)
+            h = work.tile([P, H], BF16, align_bytes=64, name="h_bf")
+            nc.vector.tensor_tensor(h[:], res[1][:], sig[:], MULT)
+            h_bf[e, s] = h
+
+        def turn(e, tiles):
+            n = len(tiles) * P
+            ps = psum.tile([P, 2, n], F32, name="ht_ps")
+            for i, s in enumerate(tiles):
+                words = h_bf[e, s][:].bitcast(F32)
+                for u in range(2):
+                    nc.tensor.transpose(ps[:, u, i * P : (i + 1) * P], words[:, u : H // 2 : 2], ident[:])
+            ht_ps[e, tiles[0]] = ps
+
+        def second(e, tiles):
+            n = len(tiles) * P
+            c0 = e * C + tiles[0] * P
+            ht = work.tile([P, n, 4], BF16, align_bytes=64, name="ht")
+            flat = ht[:].rearrange("p r d -> p (r d)")
+            nc.scalar.copy(
+                flat.bitcast(F32).rearrange("p (r u) -> p r u", u=2), ht_ps[e, tiles[0]][:].rearrange("p u r -> p r u")
+            )
+            hw = work.tile([P, n], U32, align_bytes=64, name="hw")
+            hs = work.tile([P, n], U8, align_bytes=64, name="hs")
+            nc.vector.quantize_mx(out=hw[:].bitcast(FP8X4), scales=hs[:], in_=flat)
+            yp = psum.tile([P, n], F32, name="y_ps")
+            nc.tensor.matmul_mx(
+                out=yp[:],
+                lhsT=w2[e].bitcast(FP4X4),
+                lhsT_scale=sc2[:, e * N : (e + 1) * N],
+                rhs=hw[:].bitcast(FP8X4),
+                rhs_scale=hs[:],
+                start=True,
+                stop=True,
+            )
+            nc.scalar.copy(y_all[:, c0 : c0 + n], yp[:])
+
+        both = [0, 1]
+        gather(0, 2)
+        for e in range(E - 1):
+            first(e, 0)
+            first(e, 1)
+            if e > 0:
+                second(e - 1, both)
+            gather(e + 1, 1)
+            turn(e, both)
+        e = E - 1
+        first(e, 0)
+        turn(e, [0])
+        first(e, 1)
+        second(e - 1, both)
+        turn(e, [1])
+        second(e, [0])
+        second(e, [1])
+
+        terms = []
+        for r in range(TOP):
+            t = keep.tile([P, T], F32, name=f"term{r}")
+            nc.vector.tensor_tensor(t[:], y_all[:].indirect(pos_t[r][:]), gate_t[:, r, :], MULT)
+            terms.append(t)
+        halves = [slice(0, T // 2), slice(T // 2, T)]
+        part = keep.tile([P, T], F32, name="part")
+        res = keep.tile([P, T], F32, name="res")
+        for hf in halves:
+            nc.vector.tensor_tensor(part[:, hf], terms[0][:, hf], terms[1][:, hf], ADD)
+        for hf in halves:
+            nc.vector.tensor_tensor(res[:, hf], part[:, hf], terms[2][:, hf], ADD)
+            nc.sync.dma_start(out=out[:, hf], in_=res[:, hf])

@@ -28,7 +28,7 @@ def tile_moe_tk_glu_sigmoid_kernel(
     nc = tc.nc
     with ExitStack() as ctx:
         keep = ctx.enter_context(tc.tile_pool(name="keep", bufs=1))
-        work = ctx.enter_context(tc.tile_pool(name="work", bufs=3))
+        work = ctx.enter_context(tc.tile_pool(name="work", bufs=6))
         psum = ctx.enter_context(tc.psum_pool(name="psum", bufs=2))
 
         warm = keep.tile([P, 1], F32, name="warm")
@@ -40,7 +40,7 @@ def tile_moe_tk_glu_sigmoid_kernel(
         x_raw = []
         offs_t = keep.tile([P, S // 16], U16, name="offs_t")
         nc.sync.dma_start(offs_t[:], offs)
-        x_cuts = [(0, 256), (256, 512)]
+        x_cuts = [(0, 256), (256, 384), (384, 512)]
         for c, (t0, t1) in enumerate(x_cuts):
             xr = keep.tile([P, 4, t1 - t0], F32, name=f"x_raw{c}")
             nc.sync.dma_start(out=xr[:], in_=x_view[:, :, t0:t1])
@@ -50,10 +50,10 @@ def tile_moe_tk_glu_sigmoid_kernel(
         sc3 = keep.tile([P, E * H], U8, align_bytes=64, name="sc3")
         sc2 = keep.tile([P, E * N], U8, align_bytes=64, name="sc2")
         xs = keep.tile([P, T], U8, align_bytes=64, name="xs")
-        nc.vector.memset(sc1[:].bitcast(I32), 0)
         nc.vector.memset(sc3[:].bitcast(I32), 0)
+        nc.vector.memset(sc1[:].bitcast(I32), 0)
         nc.vector.memset(sc2[:].bitcast(I32), 0)
-        nc.gpsimd.memset(xs[:], 0)
+        nc.vector.memset(xs[:].bitcast(I32), 0)
 
         def load_words(words, width, e0, e1, name, eng):
             t = keep.tile([P, (e1 - e0) * 2 * width], U8, align_bytes=64, name=name)
@@ -69,16 +69,16 @@ def tile_moe_tk_glu_sigmoid_kernel(
                     in_=src[:, 0, 4 * q : 4 * q + 4, :].rearrange("e q c -> q e c"),
                 )
 
-        w1 = load_words(w1_words, H, 0, 1, "w1_a", nc.gpsimd)
-        w3 = load_words(w3_words, H, 0, 1, "w3_a", nc.gpsimd)
+        w1 = load_words(w1_words, H, 0, 1, "w1_a", nc.sync)
+        w3 = load_words(w3_words, H, 0, 1, "w3_a", nc.sync)
+        load_scales(sc3, w3_scales, nc.gpsimd)
         load_scales(sc1, w1_scales, nc.sync)
-        load_scales(sc3, w3_scales, nc.sync)
-        load_scales(sc2, w2_scales, nc.sync)
         ident = keep.tile([P, P], F32, name="ident")
         make_identity(nc, ident[:])
-        w1 += load_words(w1_words, H, 1, 3, "w1_b", nc.gpsimd)
-        w3 += load_words(w3_words, H, 1, 3, "w3_b", nc.gpsimd)
+        w1 += load_words(w1_words, H, 1, 3, "w1_b", nc.sync)
+        w3 += load_words(w3_words, H, 1, 3, "w3_b", nc.sync)
         w2 = load_words(w2_words, N, 0, E, "w2_t", nc.gpsimd)
+        load_scales(sc2, w2_scales, nc.sync)
         w1 += load_words(w1_words, H, 3, 6, "w1_c", nc.sync)
         w3 += load_words(w3_words, H, 3, 6, "w3_c", nc.sync)
         pos_t = []
@@ -92,7 +92,7 @@ def tile_moe_tk_glu_sigmoid_kernel(
         xw = keep.tile([P, T], U32, align_bytes=64, name="xw")
         for c, (t0, t1) in enumerate(x_cuts):
             xb = keep.tile([P, t1 - t0, 4], BF16, align_bytes=64, name=f"x_bf{c}")
-            nc.vector.tensor_copy(out=xb[:], in_=x_raw[c][:].rearrange("p j t -> p t j"))
+            (nc.scalar.copy if c == 2 else nc.vector.tensor_copy)(out=xb[:], in_=x_raw[c][:].rearrange("p j t -> p t j"))
             cols = slice(t0, t1)
             nc.vector.quantize_mx(
                 out=xw[:, cols].bitcast(FP8X4), scales=xs[:, cols], in_=xb[:].rearrange("p t j -> p (t j)")
@@ -105,8 +105,8 @@ def tile_moe_tk_glu_sigmoid_kernel(
         ht_ps = {}
 
         def gather(e, pieces):
-            a = keep.tile([P, C], U32, align_bytes=64, name=f"gw{e}")
-            b = keep.tile([P, C], U8, align_bytes=64, name=f"gs{e}")
+            a = work.tile([P, C], U32, align_bytes=64, name="gw_t", bufs=3)
+            b = work.tile([P, C], U8, align_bytes=64, name="gs_t", bufs=3)
             n = C // pieces
             for i in range(pieces):
                 idx = offs_t[:, (e * C + i * n) // 16 : (e * C + (i + 1) * n) // 16]
@@ -115,25 +115,39 @@ def tile_moe_tk_glu_sigmoid_kernel(
             gw[e] = a
             gs[e] = b
 
-        def first(e, s):
+        sigs = {}
+
+        def product(e, s, w, sc, nm):
             cols = slice(s * P, (s + 1) * P)
-            res = []
-            for w, sc, nm in ((w1, sc1, "a_ps"), (w3, sc3, "b_ps")):
-                ps = psum.tile([P, H], F32, name=nm)
-                nc.tensor.matmul_mx(
-                    out=ps[:],
-                    lhsT=gw[e][:, cols].bitcast(FP8X4),
-                    lhsT_scale=gs[e][:, cols],
-                    rhs=w[e].bitcast(FP4X4),
-                    rhs_scale=sc[:, e * H : (e + 1) * H],
-                    start=True,
-                    stop=True,
-                )
-                res.append(ps)
+            ps = psum.tile([P, H], F32, name=nm)
+            nc.tensor.matmul_mx(
+                out=ps[:],
+                lhsT=gw[e][:, cols].bitcast(FP8X4),
+                lhsT_scale=gs[e][:, cols],
+                rhs=w[e].bitcast(FP4X4),
+                rhs_scale=sc[:, e * H : (e + 1) * H],
+                start=True,
+                stop=True,
+            )
+            return ps
+
+        def first_a(e, s):
+            ps = product(e, s, w1, sc1, "a_ps")
             sig = work.tile([P, H], F32, name="sig")
-            nc.scalar.activation(sig[:], res[0][:], SIGMOID)
+            nc.scalar.activation(sig[:], ps[:], SIGMOID)
+            sigs[e, s] = sig
+
+        def first_b(e, s):
+            ps = product(e, s, w3, sc3, "b_ps")
+            sig = sigs[e, s]
             h = work.tile([P, H], BF16, align_bytes=64, name="h_bf")
-            nc.vector.tensor_tensor(h[:], res[1][:], sig[:], MULT)
+            turned = "p (m u d) -> p u m d"
+            nc.vector.tensor_tensor(
+                h[:].rearrange("p (u m d) -> p u m d", u=2, d=2),
+                ps[:].rearrange(turned, u=2, d=2),
+                sig[:].rearrange(turned, u=2, d=2),
+                MULT,
+            )
             h_bf[e, s] = h
 
         def turn(e, tiles):
@@ -142,17 +156,24 @@ def tile_moe_tk_glu_sigmoid_kernel(
             for i, s in enumerate(tiles):
                 words = h_bf[e, s][:].bitcast(F32)
                 for u in range(2):
-                    nc.tensor.transpose(ps[:, u, i * P : (i + 1) * P], words[:, u : H // 2 : 2], ident[:])
+                    nc.tensor.transpose(ps[:, u, i * P : (i + 1) * P], words[:, u * P : (u + 1) * P], ident[:])
             ht_ps[e, tiles[0]] = ps
+
+        flats = {}
+
+        def lift(e, tiles):
+            n = len(tiles) * P
+            ht = work.tile([P, n, 4], BF16, align_bytes=64, name="ht")
+            flat = ht[:].rearrange("p r d -> p (r d)")
+            flats[e, tiles[0]] = flat
+            nc.scalar.copy(
+                flat.bitcast(F32).rearrange("p (r u) -> p r u", u=2), ht_ps[e, tiles[0]][:].rearrange("p u r -> p r u")
+            )
 
         def second(e, tiles):
             n = len(tiles) * P
             c0 = e * C + tiles[0] * P
-            ht = work.tile([P, n, 4], BF16, align_bytes=64, name="ht")
-            flat = ht[:].rearrange("p r d -> p (r d)")
-            nc.scalar.copy(
-                flat.bitcast(F32).rearrange("p (r u) -> p r u", u=2), ht_ps[e, tiles[0]][:].rearrange("p u r -> p r u")
-            )
+            flat = flats[e, tiles[0]]
             hw = work.tile([P, n], U32, align_bytes=64, name="hw")
             hs = work.tile([P, n], U8, align_bytes=64, name="hs")
             nc.vector.quantize_mx(out=hw[:].bitcast(FP8X4), scales=hs[:], in_=flat)
@@ -168,23 +189,16 @@ def tile_moe_tk_glu_sigmoid_kernel(
             )
             nc.scalar.copy(y_all[:, c0 : c0 + n], yp[:])
 
-        both = [0, 1]
-        gather(0, 2)
-        for e in range(E - 1):
-            first(e, 0)
-            first(e, 1)
-            if e > 0:
-                second(e - 1, both)
-            gather(e + 1, 1)
-            turn(e, both)
-        e = E - 1
-        first(e, 0)
-        turn(e, [0])
-        first(e, 1)
-        second(e - 1, both)
-        turn(e, [1])
-        second(e, [0])
-        second(e, [1])
+        for e in range(E):
+            gather(e, 2 if e == 0 else 1)
+            first_a(e, 0)
+            first_a(e, 1)
+            for tiles in ([0], [1]) if e >= 3 else ([0, 1],):
+                for s in tiles:
+                    first_b(e, s)
+                turn(e, tiles)
+                lift(e, tiles)
+                second(e, tiles)
 
         terms = []
         for r in range(TOP):

@@ -50,8 +50,8 @@ def tile_moe_tk_glu_sigmoid_kernel(
         sc3 = keep.tile([P, E * H], U8, align_bytes=64, name="sc3")
         sc2 = keep.tile([P, E * N], U8, align_bytes=64, name="sc2")
         xs = keep.tile([P, T], U8, align_bytes=64, name="xs")
-        nc.vector.memset(sc3[:].bitcast(I32), 0)
         nc.vector.memset(sc1[:].bitcast(I32), 0)
+        nc.vector.memset(sc3[:].bitcast(I32), 0)
         nc.vector.memset(sc2[:].bitcast(I32), 0)
         nc.vector.memset(xs[:].bitcast(I32), 0)
 
@@ -69,16 +69,16 @@ def tile_moe_tk_glu_sigmoid_kernel(
                     in_=src[:, 0, 4 * q : 4 * q + 4, :].rearrange("e q c -> q e c"),
                 )
 
-        w1 = load_words(w1_words, H, 0, 1, "w1_a", nc.sync)
-        w3 = load_words(w3_words, H, 0, 1, "w3_a", nc.sync)
-        load_scales(sc3, w3_scales, nc.gpsimd)
-        load_scales(sc1, w1_scales, nc.sync)
         ident = keep.tile([P, P], F32, name="ident")
         make_identity(nc, ident[:])
-        w1 += load_words(w1_words, H, 1, 3, "w1_b", nc.sync)
-        w3 += load_words(w3_words, H, 1, 3, "w3_b", nc.sync)
-        w2 = load_words(w2_words, N, 0, E, "w2_t", nc.gpsimd)
+        w1 = load_words(w1_words, H, 0, 1, "w1_a", nc.gpsimd)
+        w3 = load_words(w3_words, H, 0, 1, "w3_a", nc.gpsimd)
+        load_scales(sc1, w1_scales, nc.sync)
+        load_scales(sc3, w3_scales, nc.sync)
         load_scales(sc2, w2_scales, nc.sync)
+        w1 += load_words(w1_words, H, 1, 3, "w1_b", nc.gpsimd)
+        w3 += load_words(w3_words, H, 1, 3, "w3_b", nc.gpsimd)
+        w2 = load_words(w2_words, N, 0, E, "w2_t", nc.gpsimd)
         w1 += load_words(w1_words, H, 3, 6, "w1_c", nc.sync)
         w3 += load_words(w3_words, H, 3, 6, "w3_c", nc.sync)
         pos_t = []

from contextlib import ExitStack

import concourse.mybir as mybir
from concourse.masks import make_identity

P = 128
K, T, E, C, H, N = 512, 512, 6, 256, 512, 128
S = E * C
TOP = 3
FLOPS = 2 * S * (2 * K * H + H * N)

F32 = mybir.dt.float32
BF16 = mybir.dt.bfloat16
I32 = mybir.dt.int32
U32 = mybir.dt.uint32
U16 = mybir.dt.uint16
U8 = mybir.dt.uint8
FP8X4 = mybir.dt.float8_e4m3fn_x4
FP4X4 = mybir.dt.float4_e2m1fn_x4
SIGMOID = mybir.ActivationFunctionType.Sigmoid
MULT = mybir.AluOpType.mult
ADD = mybir.AluOpType.add


def tile_moe_tk_glu_sigmoid_kernel(
    tc, xT, w1_words, w1_scales, w3_words, w3_scales, w2_words, w2_scales, gate, offs, pos1, pos2, pos3, out
):
    nc = tc.nc
    with ExitStack() as ctx:
        keep = ctx.enter_context(tc.tile_pool(name="keep", bufs=1))
        work = ctx.enter_context(tc.tile_pool(name="work", bufs=6))
        psum = ctx.enter_context(tc.psum_pool(name="psum", bufs=2))

        warm = keep.tile([P, 1], F32, name="warm")
        nc.vector.memset(warm[:], 0.0)
        warm2 = keep.tile([P, 1], F32, name="warm2")
        nc.scalar.activation(warm2[:], warm[:], SIGMOID)

        x_view = xT.rearrange("(p j) t -> p j t", j=4)
        x_raw = []
        offs_t = keep.tile([P, S // 16], U16, name="offs_t")
        nc.sync.dma_start(offs_t[:], offs)
        x_cuts = [(0, 256), (256, 384), (384, 512)]
        for c, (t0, t1) in enumerate(x_cuts):
            xr = keep.tile([P, 4, t1 - t0], F32, name=f"x_raw{c}")
            nc.sync.dma_start(out=xr[:], in_=x_view[:, :, t0:t1])
            x_raw.append(xr)

        sc1 = keep.tile([P, E * H], U8, align_bytes=64, name="sc1")
        sc3 = keep.tile([P, E * H], U8, align_bytes=64, name="sc3")
        sc2 = keep.tile([P, E * N], U8, align_bytes=64, name="sc2")
        xs = keep.tile([P, T], U8, align_bytes=64, name="xs")
        nc.vector.memset(sc1[:].bitcast(I32), 0)
        nc.vector.memset(sc3[:].bitcast(I32), 0)
        nc.vector.memset(sc2[:].bitcast(I32), 0)
        nc.vector.memset(xs[:].bitcast(I32), 0)

        def load_words(words, width, e0, e1, name, eng):
            t = keep.tile([P, (e1 - e0) * 2 * width], U8, align_bytes=64, name=name)
            src = words.bitcast(I32)[e0:e1, 0].rearrange("e p c -> p e c")
            eng.dma_start(out=t[:].bitcast(I32).rearrange("p (e c) -> p e c", e=e1 - e0), in_=src)
            return [t[:, i * 2 * width : (i + 1) * 2 * width] for i in range(e1 - e0)]

        def load_scales(tile, scales, eng):
            src = scales.bitcast(I32)
            for q in range(4):
                eng.dma_start(
                    out=tile[:].bitcast(I32)[32 * q : 32 * q + 4, :].rearrange("p (e c) -> p e c", e=E),
                    in_=src[:, 0, 4 * q : 4 * q + 4, :].rearrange("e q c -> q e c"),
                )

        ident = keep.tile([P, P], F32, name="ident")
        make_identity(nc, ident[:])
        w1 = load_words(w1_words, H, 0, 1, "w1_a", nc.gpsimd)
        w3 = load_words(w3_words, H, 0, 1, "w3_a", nc.gpsimd)
        load_scales(sc1, w1_scales, nc.sync)
        load_scales(sc3, w3_scales, nc.sync)
        load_scales(sc2, w2_scales, nc.sync)
        w1 += load_words(w1_words, H, 1, 3, "w1_b", nc.gpsimd)
        w3 += load_words(w3_words, H, 1, 3, "w3_b", nc.gpsimd)
        w2 = load_words(w2_words, N, 0, E, "w2_t", nc.gpsimd)
        w1 += load_words(w1_words, H, 3, 6, "w1_c", nc.sync)
        w3 += load_words(w3_words, H, 3, 6, "w3_c", nc.sync)
        pos_t = []
        for r, pos in enumerate((pos1, pos2, pos3)):
            pt = keep.tile([P, T // 16], U16, name=f"pos_t{r}")
            nc.sync.dma_start(pt[:], pos)
            pos_t.append(pt)
        gate_t = keep.tile([P, TOP, T], F32, name="gate_t")
        nc.sync.dma_start(out=gate_t[:], in_=gate.rearrange("r p t -> p r t"))

        xw = keep.tile([P, T], U32, align_bytes=64, name="xw")
        for c, (t0, t1) in enumerate(x_cuts):
            xb = keep.tile([P, t1 - t0, 4], BF16, align_bytes=64, name=f"x_bf{c}")
            (nc.scalar.copy if c == 2 else nc.vector.tensor_copy)(out=xb[:], in_=x_raw[c][:].rearrange("p j t -> p t j"))
            cols = slice(t0, t1)
            nc.vector.quantize_mx(
                out=xw[:, cols].bitcast(FP8X4), scales=xs[:, cols], in_=xb[:].rearrange("p t j -> p (t j)")
            )

        y_all = keep.tile([P, S], F32, name="y_all")
        gw = {}
        gs = {}
        h_bf = {}
        ht_ps = {}

        def gather(e, pieces):
            a = work.tile([P, C], U32, align_bytes=64, name="gw_t", bufs=3)
            b = work.tile([P, C], U8, align_bytes=64, name="gs_t", bufs=3)
            n = C // pieces
            for i in range(pieces):
                idx = offs_t[:, (e * C + i * n) // 16 : (e * C + (i + 1) * n) // 16]
                nc.vector.tensor_copy(a[:, i * n : (i + 1) * n], xw[:].indirect(idx))
                nc.vector.tensor_copy(b[:, i * n : (i + 1) * n], xs[:].indirect(idx))
            gw[e] = a
            gs[e] = b

        sigs = {}

        def product(e, s, w, sc, nm):
            cols = slice(s * P, (s + 1) * P)
            ps = psum.tile([P, H], F32, name=nm)
            nc.tensor.matmul_mx(
                out=ps[:],
                lhsT=gw[e][:, cols].bitcast(FP8X4),
                lhsT_scale=gs[e][:, cols],
                rhs=w[e].bitcast(FP4X4),
                rhs_scale=sc[:, e * H : (e + 1) * H],
                start=True,
                stop=True,
            )
            return ps

        def first_a(e, s):
            ps = product(e, s, w1, sc1, "a_ps")
            sig = work.tile([P, H], F32, name="sig")
            nc.scalar.activation(sig[:], ps[:], SIGMOID)
            sigs[e, s] = sig

        def first_b(e, s):
            ps = product(e, s, w3, sc3, "b_ps")
            sig = sigs[e, s]
            h = work.tile([P, H], BF16, align_bytes=64, name="h_bf")
            turned = "p (m u d) -> p u m d"
            nc.vector.tensor_tensor(
                h[:].rearrange("p (u m d) -> p u m d", u=2, d=2),
                ps[:].rearrange(turned, u=2, d=2),
                sig[:].rearrange(turned, u=2, d=2),
                MULT,
            )
            h_bf[e, s] = h

        def turn(e, tiles):
            n = len(tiles) * P
            ps = psum.tile([P, 2, n], F32, name="ht_ps")
            for i, s in enumerate(tiles):
                words = h_bf[e, s][:].bitcast(F32)
                for u in range(2):
                    nc.tensor.transpose(ps[:, u, i * P : (i + 1) * P], words[:, u * P : (u + 1) * P], ident[:])
            ht_ps[e, tiles[0]] = ps

        flats = {}

        def lift(e, tiles):
            n = len(tiles) * P
            ht = work.tile([P, n, 4], BF16, align_bytes=64, name="ht")
            flat = ht[:].rearrange("p r d -> p (r d)")
            flats[e, tiles[0]] = flat
            nc.scalar.copy(
                flat.bitcast(F32).rearrange("p (r u) -> p r u", u=2), ht_ps[e, tiles[0]][:].rearrange("p u r -> p r u")
            )

        def second(e, tiles):
            n = len(tiles) * P
            c0 = e * C + tiles[0] * P
            flat = flats[e, tiles[0]]
            hw = work.tile([P, n], U32, align_bytes=64, name="hw")
            hs = work.tile([P, n], U8, align_bytes=64, name="hs")
            nc.vector.quantize_mx(out=hw[:].bitcast(FP8X4), scales=hs[:], in_=flat)
            yp = psum.tile([P, n], F32, name="y_ps")
            nc.tensor.matmul_mx(
                out=yp[:],
                lhsT=w2[e].bitcast(FP4X4),
                lhsT_scale=sc2[:, e * N : (e + 1) * N],
                rhs=hw[:].bitcast(FP8X4),
                rhs_scale=hs[:],
                start=True,
                stop=True,
            )
            nc.scalar.copy(y_all[:, c0 : c0 + n], yp[:])

        for e in range(E):
            gather(e, 2 if e == 0 else 1)
            first_a(e, 0)
            first_a(e, 1)
            for tiles in ([0], [1]) if e >= 3 else ([0, 1],):
                for s in tiles:
                    first_b(e, s)
                turn(e, tiles)
                lift(e, tiles)
                second(e, tiles)

        terms = []
        for r in range(TOP):
            t = keep.tile([P, T], F32, name=f"term{r}")
            nc.vector.tensor_tensor(t[:], y_all[:].indirect(pos_t[r][:]), gate_t[:, r, :], MULT)
            terms.append(t)
        halves = [slice(0, T // 2), slice(T // 2, T)]
        part = keep.tile([P, T], F32, name="part")
        res = keep.tile([P, T], F32, name="res")
        for hf in halves:
            nc.vector.tensor_tensor(part[:, hf], terms[0][:, hf], terms[1][:, hf], ADD)
        for hf in halves:
            nc.vector.tensor_tensor(res[:, hf], part[:, hf], terms[2][:, hf], ADD)
            nc.sync.dma_start(out=out[:, hf], in_=res[:, hf])
